import numpy as np
import ml_dtypes


def mxq(x, axis, fmt="e4m3"):
    dtype, down = {"e4m3": (ml_dtypes.float8_e4m3fn, 7), "e5m2": (ml_dtypes.float8_e5m2, 14)}[fmt]
    v = np.moveaxis(np.asarray(x, np.float32).astype(ml_dtypes.bfloat16).astype(np.float64), axis, -1)
    blocks = v.reshape(v.shape[:-1] + (-1, 32))
    amax = np.abs(blocks).max(-1, keepdims=True)
    byte = np.maximum(np.where(amax > 0, np.frexp(amax)[1] - 1 + 127, 0) - down, 1)
    scale = np.exp2(byte - 127.0)
    codes = (blocks / scale).astype(np.float32).astype(dtype).astype(np.float64)
    return np.moveaxis((codes * scale).reshape(v.shape), -1, axis)


WIDE = False


def mx_kscale(k):
    if not WIDE:
        return np.ones(k)
    levels = np.array([10, -10, 5, -5, 0])
    if k % 512:
        return np.exp2(np.random.permutation(np.resize(levels, k // 32))).repeat(32)
    a = np.empty((k // 512, 16))
    for p in range(k // 512):
        a[p, :8] = np.random.permutation(np.resize(levels, 8))
        for g in range(8):
            far = levels[np.abs(levels - a[p, g]) >= 10]
            a[p, g + 8] = far[np.random.randint(len(far))]
    return np.exp2(a.ravel()).repeat(32)


def f64(x):
    return np.asarray(x).astype(np.float64)


def striped(idx):
    return np.tile(idx.reshape(-1, 16).T, (8, 1)).astype(np.uint16)


def unstriped(offs):
    return offs[:16].T.reshape(-1).astype(np.int64)


E2M1 = np.array([0.0, 0.5, 1.0, 1.5, 2.0, 3.0, 4.0, 6.0, -0.0, -0.5, -1.0, -1.5, -2.0, -3.0, -4.0, -6.0])


def pack_weight(w, fmt):
    k, n = w.shape
    w = f64(np.asarray(w, np.float32).astype(ml_dtypes.bfloat16)).reshape(k // 32, 32, n)
    amax = np.abs(w).max(1)
    if fmt == "e4m3":
        byte = np.frexp(amax)[1] - 1 + 127 - 7
    else:
        mant, ex = np.frexp(amax / 6.0)
        byte = np.where(mant > 0.5, ex, ex - 1) + 127
    byte = np.clip(np.where(amax > 0, byte, 1), 1, 254)
    scaled = (w * np.exp2(127.0 - byte)[:, None, :]).reshape(k, n).astype(np.float32)
    by_word = np.ascontiguousarray(scaled.reshape(k // 512, 128, 4, n).transpose(0, 1, 3, 2))
    if fmt == "e4m3":
        words = by_word.astype(ml_dtypes.float8_e4m3fn).view(np.uint8)
    else:
        c = by_word.astype(ml_dtypes.float4_e2m1fn).view(np.uint8) & 0xF
        words = (c[..., 0::2] | (c[..., 1::2] << 4)).reshape(k // 512, 128, 2 * n)
    return np.ascontiguousarray(words), np.ascontiguousarray(byte.astype(np.uint8).reshape(k // 512, 16, n))


def unpack_weight(words, scales, fmt):
    g, _, n = scales.shape
    words = np.ascontiguousarray(words).reshape(g, 128, n, -1)
    if fmt == "e4m3":
        vals = words.view(ml_dtypes.float8_e4m3fn).astype(np.float64)
    else:
        nib = np.empty((g, 128, n, 4), np.uint8)
        nib[..., 0::2] = words & 0xF
        nib[..., 1::2] = words >> 4
        vals = E2M1[nib]
    vals = vals * np.repeat(np.exp2(scales.astype(np.float64) - 127.0), 8, axis=1)[..., None]
    return vals.transpose(0, 1, 3, 2).reshape(g * 512, n)


def gelu(v):
    return 0.5 * v * (1.0 + np.tanh(np.sqrt(2.0 / np.pi) * (v + 0.044715 * v**3)))


K, T, S, P, H = 1536, 4096, 1024, 512, 512

def setup_inputs():
    n = np.random.standard_normal
    s = mx_kscale(K)[:, None]
    u = mx_kscale(H)[:, None]
    tab_words, tab_scales = pack_weight(n((K, T)) * s, "e4m3")
    w4_words, w4_scales = pack_weight(0.78 * n((K, H)) / np.sqrt(K) / s, "e2m1")
    w3_words, w3_scales = pack_weight(n((H, H)) / np.sqrt(H) / u, "e4m3")
    perm = np.random.permutation(S)
    return {
        "tab_words": tab_words, "tab_scales": tab_scales,
        "offs": striped(np.random.permutation(T)[:S]),
        "pos1": striped(perm[:P]), "pos2": striped(perm[P:]),
        "w1": (0.78 * n((K, H)) / np.sqrt(K) / s).astype(np.float32),
        "w4_words": w4_words, "w4_scales": w4_scales,
        "w3_words": w3_words, "w3_scales": w3_scales,
        "depth": np.random.uniform(0.4, 1.6, (H, S)).astype(np.float32),
        "slope": np.random.uniform(1, 3, H).astype(np.float32),
        "share": np.random.uniform(0.1, 0.5, H).astype(np.float32),
        "wear": (0.3 * n((H, P))).astype(np.float32),
        "skip": np.random.uniform(0.4, 1.0, H).astype(np.float32),
        "wgs": np.exp(0.3 * n((128, P))).astype(np.float32),
        "gain": (np.random.uniform(1.0, 2.5, H) * u[:, 0]).astype(np.float32),
        "room": (0.4 * n((H, S))).astype(np.float32),
    }

def reference(tab_words, tab_scales, offs, pos1, pos2, w1, w4_words, w4_scales, w3_words, w3_scales,
              depth, slope, share, wear, skip, wgs, gain, room):
    v = unpack_weight(tab_words, tab_scales, "e4m3")[:, unstriped(offs)]
    w4 = unpack_weight(w4_words, w4_scales, "e2m1")
    w3 = unpack_weight(w3_words, w3_scales, "e4m3")
    x = f64(depth) * (mxq(f64(w1), 0, "e4m3").T @ v)
    h = np.maximum(x, w4.T @ v)
    top = h.max(axis=1)
    a = 1.0 / (1.0 + np.exp(-f64(slope)[:, None] * (h[:, unstriped(pos1)] - f64(share)[:, None] * top[:, None])))
    a = a - f64(wear)
    page = f64(skip)[:, None] * h
    page[:, unstriped(pos2)] = np.tile(f64(wgs), (H // 128, 1)) * a
    b = mxq(f64(gain)[:, None] * page, 0, "e4m3")
    y = w3.T @ b
    return y * h + f64(room)

@@ -1,0 +1,307 @@
+from contextlib import ExitStack
+
+import concourse.mybir as mybir
+
+K, T, S, PICK, H = 1536, 4096, 1024, 512, 512
+FLOPS = 2 * 2 * K * H * S + 2 * H * H * S
+
+F32 = mybir.dt.float32
+BF16 = mybir.dt.bfloat16
+I32 = mybir.dt.int32
+U32 = mybir.dt.uint32
+U16 = mybir.dt.uint16
+U8 = mybir.dt.uint8
+FP8X4 = mybir.dt.float8_e4m3fn_x4
+FP4X4 = mybir.dt.float4_e2m1fn_x4
+ACT = mybir.ActivationFunctionType
+ALU = mybir.AluOpType
+AXIS = mybir.AxisListType
+
+P = 128
+PACK = 4
+PASSES = K // (P * PACK)
+QUADS = 4
+BANK = 512
+READ_OUT = ((0, 256), (256, 256), (512, 512))
+
+
+def tile_list_crease_bridge_features_kernel(
+    tc, tab_words, tab_scales, offs, pos1, pos2, w1, w4_words, w4_scales, w3_words, w3_scales,
+    depth, slope, share, wear, skip, wgs, gain, room, out,
+):
+    nc = tc.nc
+    with ExitStack() as ctx:
+        lists = ctx.enter_context(tc.tile_pool(name="lists", bufs=1))
+        keep = ctx.enter_context(tc.tile_pool(name="keep", bufs=1))
+        big = ctx.enter_context(tc.tile_pool(name="big", bufs=PASSES))
+        ring = ctx.enter_context(tc.tile_pool(name="ring", bufs=2))
+        psum = ctx.enter_context(tc.psum_pool(name="psum", bufs=1))
+
+        def bank(n, name):
+            return psum.tile([P, BANK], F32, name=name, tag="bank%d" % n)
+
+        def by_row(matrix):
+            return matrix.rearrange("(p i) c -> p i c", i=PACK)
+
+        tab_scale_rows = keep.tile([P, T], U8, name="tab_scale_rows")
+        w4_scale_raw = keep.tile([P, PASSES, H], U8, name="w4_scale_raw")
+        w3_scale_raw = keep.tile([P, H], U8, name="w3_scale_raw")
+        v_scales = keep.tile([P, PASSES, S], U8, name="v_scales", align_bytes=64)
+        nc.vector.memset(tab_scale_rows[:].bitcast(I32), 0)
+        nc.gpsimd.memset(w4_scale_raw[:].bitcast(I32), 0)
+        nc.vector.memset(v_scales[:].bitcast(I32), 0)
+        nc.vector.memset(w3_scale_raw[:].bitcast(I32), 0)
+        for q in range(QUADS):
+            nc.gpsimd.dma_start(
+                out=w4_scale_raw[32 * q : 32 * q + 4, :, :].bitcast(I32),
+                in_=w4_scales[:, 4 * q : 4 * q + 4, :].rearrange("a r c -> r a c").bitcast(I32),
+            )
+
+        offs_sb = lists.tile([P, S // 16], U16, name="offs_sb")
+        pos1_sb = lists.tile([P, PICK // 16], U16, name="pos1_sb")
+        pos2_sb = lists.tile([P, PICK // 16], U16, name="pos2_sb")
+        nc.sync.dma_start(offs_sb[:], offs)
+
+        w4_raw = keep.tile([P, PASSES, 2 * H], U8, name="w4_raw")
+        nc.sync.dma_start(out=w4_raw[:].bitcast(I32), in_=w4_words.rearrange("a p c -> p a c").bitcast(I32))
+        live_rows = PASSES * 16
+        nc.scalar.dma_start(
+            out=tab_scale_rows[0:live_rows, :].bitcast(I32),
+            in_=tab_scales.rearrange("a q t -> q a t").bitcast(I32),
+        )
+
+        tab = []
+        w1_raw = []
+
+        def load_tab(a):
+            words = big.tile([P, T], U32, name="tab%d" % a, tag="big")
+            nc.sync.dma_start(out=words[:].bitcast(I32), in_=tab_words[a].rearrange("p t i -> p (t i)").bitcast(I32))
+            tab.append(words)
+
+        def load_w1(a, halves):
+            width = H // halves
+            parts = []
+            for u in range(halves):
+                part = keep.tile([P, PACK, width], F32, name="w1_raw%d_%d" % (a, u))
+                rows = w1[P * PACK * a : P * PACK * (a + 1), u * width : (u + 1) * width]
+                nc.sync.dma_start(out=part[:], in_=by_row(rows))
+                parts.append(part)
+            w1_raw.append(parts)
+
+        load_tab(0)
+        load_w1(0, 1)
+        row_values = {}
+        for name, vec in (("slope", slope), ("share", share), ("skip", skip), ("gain", gain)):
+            row_values[name] = keep.tile([P, PACK], F32, name=name + "_sb")
+            nc.sync.dma_start(out=row_values[name][:], in_=vec.rearrange("(p i) -> p i", i=PACK))
+        load_tab(1)
+        load_w1(1, 1)
+        for q in range(QUADS):
+            nc.sync.dma_start(
+                out=w3_scale_raw[32 * q : 32 * q + 4, :].bitcast(I32),
+                in_=w3_scales[0, 4 * q : 4 * q + 4, :].bitcast(I32),
+            )
+        load_tab(2)
+        load_w1(2, 2)
+
+        depth_sb = big.tile([P, PACK, S], F32, name="depth_sb", tag="big")
+        wear_sb = keep.tile([P, PACK, PICK], F32, name="wear_sb")
+        wgs_sb = keep.tile([P, PACK, PICK], F32, name="wgs_sb")
+        w3_raw = keep.tile([P, H], U32, name="w3_raw")
+        room_sb = big.tile([P, PACK, S], F32, name="room_sb", tag="big")
+        nc.sync.dma_start(out=depth_sb[:, 0, :], in_=by_row(depth)[:, 0, :])
+        nc.sync.dma_start(pos1_sb[:], pos1)
+        nc.sync.dma_start(out=depth_sb[:, 1, :], in_=by_row(depth)[:, 1, :])
+        nc.sync.dma_start(out=wear_sb[:, 0, :], in_=by_row(wear)[:, 0, :])
+        nc.sync.dma_start(pos2_sb[:], pos2)
+        for q in range(QUADS):
+            nc.sync.dma_start(out=wgs_sb[32 * q : 32 * q + 32, :, :], in_=by_row(wgs))
+        nc.sync.dma_start(out=wear_sb[:, 1, :], in_=by_row(wear)[:, 1, :])
+        for i in range(2, PACK):
+            nc.sync.dma_start(out=depth_sb[:, i, :], in_=by_row(depth)[:, i, :])
+            nc.sync.dma_start(out=wear_sb[:, i, :], in_=by_row(wear)[:, i, :])
+        nc.sync.dma_start(out=w3_raw[:].bitcast(I32), in_=w3_words[0].rearrange("p c i -> p (c i)").bitcast(I32))
+        nc.sync.dma_start(out=room_sb[:], in_=by_row(room))
+
+        picked_scale_rows = keep.tile([P, S], U8, name="picked_scale_rows")
+        nc.vector.tensor_copy(out=picked_scale_rows[:], in_=tab_scale_rows[:].indirect(offs_sb[:]))
+        rows_a_quad = 4 * PASSES
+        for q in range(QUADS):
+            nc.gpsimd.dma_start(
+                out=v_scales[32 * q : 32 * q + 4, :, :].bitcast(I32),
+                in_=picked_scale_rows[rows_a_quad * q : rows_a_quad * (q + 1), :].bitcast(I32),
+            )
+
+        w4_codes = keep.tile([P, PASSES, 2 * H], U8, name="w4_codes", align_bytes=64)
+        w4_scale = keep.tile([P, PASSES, H], U8, name="w4_scale", align_bytes=64)
+        w3_codes = keep.tile([P, H], U32, name="w3_codes", align_bytes=64)
+        w3_scale = keep.tile([P, H], U8, name="w3_scale", align_bytes=64)
+        nc.vector.tensor_copy(
+            out=w4_codes[:].bitcast(U16).rearrange("p a (i m) -> p a i m", i=PACK),
+            in_=w4_raw[:].bitcast(U16).rearrange("p a (m i) -> p a i m", i=PACK),
+        )
+        nc.vector.tensor_copy(
+            out=w4_scale[:].rearrange("p a (i m) -> p a i m", i=PACK),
+            in_=w4_scale_raw[:].rearrange("p a (m i) -> p a i m", i=PACK),
+        )
+
+        v_codes, w1_codes, w1_scale = [], [], []
+        for a in range(PASSES):
+            picked = keep.tile([P, S], U32, name="v_codes%d" % a, align_bytes=64)
+            nc.vector.tensor_copy(out=picked[:], in_=tab[a][:].indirect(offs_sb[:]))
+            v_codes.append(picked)
+
+            if a == 1:
+                open_at = keep.tile([P, PACK], F32, name="open_at")
+                nc.vector.scalar_tensor_tensor(
+                    out=open_at[:], in0=row_values["slope"][:], scalar=-1.0, in1=row_values["share"][:],
+                    op0=ALU.mult, op1=ALU.mult,
+                )
+                nc.vector.tensor_copy(
+                    out=w3_scale[:].rearrange("p (i m) -> p i m", i=PACK),
+                    in_=w3_scale_raw[:].rearrange("p (m i) -> p i m", i=PACK),
+                )
+            grouped = keep.tile([P, PACK, P, PACK], BF16, name="w1_grouped%d" % a, align_bytes=64)
+            halves = len(w1_raw[a])
+            for u, part in enumerate(w1_raw[a]):
+                m_cols = slice(u * P // halves, (u + 1) * P // halves)
+                copy = nc.scalar.copy if u == 0 else nc.vector.tensor_copy
+                copy(
+                    out=grouped[:, :, m_cols, :].rearrange("p i m j -> p m j i"),
+                    in_=part[:].rearrange("p j (m i) -> p m j i", i=PACK),
+                )
+            codes = keep.tile([P, H], U32, name="w1_codes%d" % a, align_bytes=64)
+            scales = keep.tile([P, H], U8, name="w1_scale%d" % a, align_bytes=64)
+            step = PACK if a < PASSES - 1 else 1
+            for i in range(0, PACK, step):
+                cols = slice(i * P, (i + step) * P)
+                nc.vector.quantize_mx(
+                    out=codes[:, cols].bitcast(FP8X4), scales=scales[:, cols],
+                    in_=grouped[:, i : i + step, :, :].rearrange("p i m j -> p (i m j)"),
+                )
+            w1_codes.append(codes)
+            w1_scale.append(scales)
+
+        h = [keep.tile([P, S], F32, name="h%d" % i) for i in range(PACK)]
+        top = keep.tile([P, PACK], F32, name="top")
+        look_bias = keep.tile([P, PACK], F32, name="look_bias")
+        page_grouped = [
+            keep.tile([P, width, PACK], BF16, name="page_grouped%d" % n, align_bytes=64)
+            for n, (start, width) in enumerate(READ_OUT)
+        ]
+        looks, pages = {}, {}
+
+        def features(i):
+            cols = slice(i * P, (i + 1) * P)
+            halves = range(S // BANK)
+            by_w1 = [bank(4 * (i % 2) + c, "by_w1_%d_%d" % (i, c)) for c in halves]
+            by_w4 = [bank(4 * (i % 2) + 2 + c, "by_w4_%d_%d" % (i, c)) for c in halves]
+            for a in range(PASSES):
+                for c in halves:
+                    j_cols = slice(c * BANK, (c + 1) * BANK)
+                    nc.tensor.matmul_mx(
+                        out=by_w4[c][:], lhsT=w4_codes[:, a, 2 * i * P : 2 * (i + 1) * P].bitcast(FP4X4),
+                        lhsT_scale=w4_scale[:, a, cols], rhs=v_codes[a][:, j_cols].bitcast(FP8X4),
+                        rhs_scale=v_scales[:, a, j_cols], start=(a == 0), stop=(a == PASSES - 1),
+                    )
+                for c in halves:
+                    j_cols = slice(c * BANK, (c + 1) * BANK)
+                    nc.tensor.matmul_mx(
+                        out=by_w1[c][:], lhsT=w1_codes[a][:, cols].bitcast(FP8X4),
+                        lhsT_scale=w1_scale[a][:, cols], rhs=v_codes[a][:, j_cols].bitcast(FP8X4),
+                        rhs_scale=v_scales[:, a, j_cols], start=(a == 0), stop=(a == PASSES - 1),
+                    )
+            deep = [ring.tile([P, BANK], F32, name="deep%d_%d" % (i, c), tag="deep") for c in halves]
+            for c in halves:
+                nc.vector.tensor_tensor(
+                    out=deep[c][:], in0=by_w1[c][:], in1=depth_sb[:, i, c * BANK : (c + 1) * BANK], op=ALU.mult
+                )
+            for c in halves:
+                nc.vector.tensor_tensor(
+                    out=h[i][:, c * BANK : (c + 1) * BANK], in0=by_w4[c][:], in1=deep[c][:], op=ALU.max
+                )
+            nc.vector.reduce_max(out=top[:, i : i + 1], in_=h[i][:], axis=AXIS.X)
+            nc.scalar.activation(
+                out=look_bias[:, i : i + 1], in_=top[:, i : i + 1], func=ACT.Copy, scale=open_at[:, i : i + 1]
+            )
+            looks[i] = ring.tile([P, PICK], F32, name="look%d" % i, tag="look")
+            nc.scalar.activation(
+                out=looks[i][:], in_=h[i][:].indirect(pos1_sb[:]), func=ACT.Sigmoid,
+                bias=look_bias[:, i : i + 1], scale=row_values["slope"][:, i : i + 1],
+            )
+            pages[i] = ring.tile([P, S], F32, name="page%d" % i, tag="page", bufs=3)
+            nc.scalar.activation(
+                out=pages[i][:], in_=h[i][:], func=ACT.Copy, scale=row_values["skip"][:, i : i + 1]
+            )
+
+        def rewrite(i):
+            worn = ring.tile([P, PICK], F32, name="worn%d" % i, tag="worn")
+            engine = nc.vector
+            engine.tensor_tensor(out=worn[:], in0=looks[i][:], in1=wear_sb[:, i, :], op=ALU.subtract)
+            nc.vector.tensor_tensor(
+                out=pages[i][:].indirect(pos2_sb[:]), in0=worn[:], in1=wgs_sb[:, i, :], op=ALU.mult
+            )
+            for n, (start, width) in enumerate(READ_OUT):
+                nc.scalar.activation(
+                    out=page_grouped[n][:, :, i], in_=pages[i][:, start : start + width], func=ACT.Copy,
+                    scale=row_values["gain"][:, i : i + 1],
+                )
+
+        features(0)
+        for i in range(1, PACK):
+            features(i)
+            if i == 1:
+                nc.scalar.copy(
+                    out=w3_codes[:].rearrange("p (i m) -> p i m", i=PACK),
+                    in_=w3_raw[:].rearrange("p (m i) -> p i m", i=PACK),
+                )
+            rewrite(i - 1)
+        rewrite(PACK - 1)
+
+        def read_out_products(n, first_bank, tag):
+            start, width = READ_OUT[n]
+            codes = keep.tile([P, width], U32, name="page_codes%d" % n, tag=tag, align_bytes=64)
+            scales = keep.tile([P, width], U8, name="page_scale%d" % n, align_bytes=64)
+            nc.vector.quantize_mx(
+                out=codes[:].bitcast(FP8X4), scales=scales[:],
+                in_=page_grouped[n][:].rearrange("p j i -> p (j i)"),
+            )
+            per_bank = BANK // width
+            sums = []
+            for i in range(PACK):
+                if i % per_bank == 0:
+                    acc = bank(first_bank + i // per_bank, "read_out%d_%d" % (n, i))
+                place = acc[:, (i % per_bank) * width : (i % per_bank + 1) * width]
+                nc.tensor.matmul_mx(
+                    out=place, lhsT=w3_codes[:, i * P : (i + 1) * P].bitcast(FP8X4),
+                    lhsT_scale=w3_scale[:, i * P : (i + 1) * P], rhs=codes[:].bitcast(FP8X4),
+                    rhs_scale=scales[:], start=True, stop=True,
+                )
+                sums.append(place)
+            return sums
+
+        def times_h(n, sums):
+            start, width = READ_OUT[n]
+            scaled = keep.tile([P, PACK, width], F32, name="scaled%d" % n, tag="scaled%d" % n, align_bytes=64)
+            for i in range(PACK):
+                nc.vector.tensor_tensor(
+                    out=scaled[:, i, :], in0=sums[i], in1=h[i][:, start : start + width], op=ALU.mult
+                )
+            return scaled
+
+        def plus_room(n, scaled, rows, engine):
+            start, width = READ_OUT[n]
+            place = room_sb[:, rows, start : start + width]
+            engine.tensor_tensor(out=place, in0=scaled[:, rows, :], in1=place, op=ALU.add)
+            nc.sync.dma_start(out=by_row(out)[:, rows, start : start + width], in_=place)
+
+        sums0 = read_out_products(0, 0, "codes0")
+        sums1 = read_out_products(1, 2, "codes1")
+        scaled0 = times_h(0, sums0)
+        plus_room(0, scaled0, slice(0, PACK), nc.vector)
+        sums2 = read_out_products(2, 4, "scaled0")
+        scaled1 = times_h(1, sums1)
+        plus_room(1, scaled1, slice(0, PACK), nc.vector)
+        scaled2 = times_h(2, sums2)
+        for i in range(PACK):
+            plus_room(2, scaled2, slice(i, i + 1), nc.vector)

@@ -33,7 +33,6 @@ def tile_list_crease_bridge_features_kernel(
     with ExitStack() as ctx:
         lists = ctx.enter_context(tc.tile_pool(name="lists", bufs=1))
         keep = ctx.enter_context(tc.tile_pool(name="keep", bufs=1))
-        big = ctx.enter_context(tc.tile_pool(name="big", bufs=PASSES))
         ring = ctx.enter_context(tc.tile_pool(name="ring", bufs=2))
         psum = ctx.enter_context(tc.psum_pool(name="psum", bufs=1))
 
@@ -43,94 +42,71 @@ def tile_list_crease_bridge_features_kernel(
         def by_row(matrix):
             return matrix.rearrange("(p i) c -> p i c", i=PACK)
 
-        tab_scale_rows = keep.tile([P, T], U8, name="tab_scale_rows")
-        w4_scale_raw = keep.tile([P, PASSES, H], U8, name="w4_scale_raw")
-        w3_scale_raw = keep.tile([P, H], U8, name="w3_scale_raw")
+        tab_scale_rows = keep.tile([P, T], U8, name="tab_scale_rows", tag="chain_a", align_bytes=64)
+        w4_scale_raw = keep.tile([P, PASSES, H], U8, name="w4_scale_raw", tag="chain_b", align_bytes=64)
         v_scales = keep.tile([P, PASSES, S], U8, name="v_scales", align_bytes=64)
         nc.vector.memset(tab_scale_rows[:].bitcast(I32), 0)
         nc.gpsimd.memset(w4_scale_raw[:].bitcast(I32), 0)
         nc.vector.memset(v_scales[:].bitcast(I32), 0)
-        nc.vector.memset(w3_scale_raw[:].bitcast(I32), 0)
-        for q in range(QUADS):
-            nc.gpsimd.dma_start(
-                out=w4_scale_raw[32 * q : 32 * q + 4, :, :].bitcast(I32),
-                in_=w4_scales[:, 4 * q : 4 * q + 4, :].rearrange("a r c -> r a c").bitcast(I32),
-            )
 
         offs_sb = lists.tile([P, S // 16], U16, name="offs_sb")
         pos1_sb = lists.tile([P, PICK // 16], U16, name="pos1_sb")
         pos2_sb = lists.tile([P, PICK // 16], U16, name="pos2_sb")
-        nc.sync.dma_start(offs_sb[:], offs)
+        row_values = {}
 
-        w4_raw = keep.tile([P, PASSES, 2 * H], U8, name="w4_raw")
-        nc.sync.dma_start(out=w4_raw[:].bitcast(I32), in_=w4_words.rearrange("a p c -> p a c").bitcast(I32))
-        live_rows = PASSES * 16
-        nc.scalar.dma_start(
-            out=tab_scale_rows[0:live_rows, :].bitcast(I32),
-            in_=tab_scales.rearrange("a q t -> q a t").bitcast(I32),
-        )
-
-        tab = []
-        w1_raw = []
-
-        def load_tab(a):
-            words = big.tile([P, T], U32, name="tab%d" % a, tag="big")
+        def load_tab(a, tag):
+            words = keep.tile([P, T], U32, name="tab%d" % a, tag=tag, align_bytes=64)
             nc.sync.dma_start(out=words[:].bitcast(I32), in_=tab_words[a].rearrange("p t i -> p (t i)").bitcast(I32))
-            tab.append(words)
+            return words
 
-        def load_w1(a, halves):
-            width = H // halves
+        def load_w1(a, tags):
+            width = H // len(tags)
             parts = []
-            for u in range(halves):
-                part = keep.tile([P, PACK, width], F32, name="w1_raw%d_%d" % (a, u))
+            for u, tag in enumerate(tags):
+                part = keep.tile([P, PACK, width], F32, name="w1_raw%d_%d" % (a, u), tag=tag, align_bytes=64)
                 rows = w1[P * PACK * a : P * PACK * (a + 1), u * width : (u + 1) * width]
                 nc.sync.dma_start(out=part[:], in_=by_row(rows))
                 parts.append(part)
-            w1_raw.append(parts)
+            return parts
 
-        load_tab(0)
-        load_w1(0, 1)
-        row_values = {}
-        for name, vec in (("slope", slope), ("share", share), ("skip", skip), ("gain", gain)):
-            row_values[name] = keep.tile([P, PACK], F32, name=name + "_sb")
-            nc.sync.dma_start(out=row_values[name][:], in_=vec.rearrange("(p i) -> p i", i=PACK))
-        load_tab(1)
-        load_w1(1, 1)
-        for q in range(QUADS):
-            nc.sync.dma_start(
-                out=w3_scale_raw[32 * q : 32 * q + 4, :].bitcast(I32),
-                in_=w3_scales[0, 4 * q : 4 * q + 4, :].bitcast(I32),
-            )
-        load_tab(2)
-        load_w1(2, 2)
-
-        depth_sb = big.tile([P, PACK, S], F32, name="depth_sb", tag="big")
-        wear_sb = keep.tile([P, PACK, PICK], F32, name="wear_sb")
-        wgs_sb = keep.tile([P, PACK, PICK], F32, name="wgs_sb")
-        w3_raw = keep.tile([P, H], U32, name="w3_raw")
-        room_sb = big.tile([P, PACK, S], F32, name="room_sb", tag="big")
-        nc.sync.dma_start(out=depth_sb[:, 0, :], in_=by_row(depth)[:, 0, :])
+        tab = [keep.tile([P, T], U32, name="tab0", align_bytes=64)]
+        tab0_words = tab_words[0].rearrange("p t i -> p (t i)").bitcast(I32)
+        for u in range(4):
+            cols = slice(u * T // 4, (u + 1) * T // 4)
+            nc.sync.dma_start(out=tab[0][:, cols].bitcast(I32), in_=tab0_words[:, cols])
+            if u == 0:
+                nc.sync.dma_start(offs_sb[:], offs)
+        w4_raw = keep.tile([P, PASSES, 2 * H], U8, name="w4_raw")
+        nc.sync.dma_start(out=w4_raw[:].bitcast(I32), in_=w4_words.rearrange("a p c -> p a c").bitcast(I32))
         nc.sync.dma_start(pos1_sb[:], pos1)
-        nc.sync.dma_start(out=depth_sb[:, 1, :], in_=by_row(depth)[:, 1, :])
-        nc.sync.dma_start(out=wear_sb[:, 0, :], in_=by_row(wear)[:, 0, :])
         nc.sync.dma_start(pos2_sb[:], pos2)
-        for q in range(QUADS):
-            nc.sync.dma_start(out=wgs_sb[32 * q : 32 * q + 32, :, :], in_=by_row(wgs))
-        nc.sync.dma_start(out=wear_sb[:, 1, :], in_=by_row(wear)[:, 1, :])
-        for i in range(2, PACK):
-            nc.sync.dma_start(out=depth_sb[:, i, :], in_=by_row(depth)[:, i, :])
-            nc.sync.dma_start(out=wear_sb[:, i, :], in_=by_row(wear)[:, i, :])
-        nc.sync.dma_start(out=w3_raw[:].bitcast(I32), in_=w3_words[0].rearrange("p c i -> p (c i)").bitcast(I32))
-        nc.sync.dma_start(out=room_sb[:], in_=by_row(room))
+        live_rows = PASSES * 16
+        nc.sync.dma_start(
+            out=tab_scale_rows[0 : 2 * live_rows : 2, :].bitcast(I32),
+            in_=tab_scales.rearrange("a q t -> q a t").bitcast(I32),
+        )
+        w1_raw = [load_w1(0, ["w1_raw0"])]
+        for r in range(4):
+            nc.sync.dma_start(
+                out=w4_scale_raw[r:P:32, :, :].bitcast(I32),
+                in_=w4_scales[:, r:16:4, :].rearrange("a q c -> q a c").bitcast(I32),
+            )
+        tab.append(load_tab(1, "chain_c"))
 
         picked_scale_rows = keep.tile([P, S], U8, name="picked_scale_rows")
         nc.vector.tensor_copy(out=picked_scale_rows[:], in_=tab_scale_rows[:].indirect(offs_sb[:]))
+        w1_raw.append(load_w1(1, ["chain_a"]))
         rows_a_quad = 4 * PASSES
-        for q in range(QUADS):
-            nc.gpsimd.dma_start(
+        for q in (0, 2, 1, 3):
+            nc.sync.dma_start(
                 out=v_scales[32 * q : 32 * q + 4, :, :].bitcast(I32),
-                in_=picked_scale_rows[rows_a_quad * q : rows_a_quad * (q + 1), :].bitcast(I32),
+                in_=picked_scale_rows[2 * rows_a_quad * q : 2 * rows_a_quad * (q + 1) : 2, :].bitcast(I32),
             )
+        tab.append(load_tab(2, "chain_b"))
+        grouped_w1 = [
+            keep.tile([P, PACK, P, PACK], BF16, name="w1_grouped%d" % a, tag="grouped%d" % a, align_bytes=64)
+            for a in range(PASSES)
+        ]
 
         w4_codes = keep.tile([P, PASSES, 2 * H], U8, name="w4_codes", align_bytes=64)
         w4_scale = keep.tile([P, PASSES, H], U8, name="w4_scale", align_bytes=64)
@@ -146,22 +122,13 @@ def tile_list_crease_bridge_features_kernel(
         )
 
         v_codes, w1_codes, w1_scale = [], [], []
-        for a in range(PASSES):
+
+        def prepare_pass(a):
             picked = keep.tile([P, S], U32, name="v_codes%d" % a, align_bytes=64)
             nc.vector.tensor_copy(out=picked[:], in_=tab[a][:].indirect(offs_sb[:]))
             v_codes.append(picked)
 
-            if a == 1:
-                open_at = keep.tile([P, PACK], F32, name="open_at")
-                nc.vector.scalar_tensor_tensor(
-                    out=open_at[:], in0=row_values["slope"][:], scalar=-1.0, in1=row_values["share"][:],
-                    op0=ALU.mult, op1=ALU.mult,
-                )
-                nc.vector.tensor_copy(
-                    out=w3_scale[:].rearrange("p (i m) -> p i m", i=PACK),
-                    in_=w3_scale_raw[:].rearrange("p (m i) -> p i m", i=PACK),
-                )
-            grouped = keep.tile([P, PACK, P, PACK], BF16, name="w1_grouped%d" % a, align_bytes=64)
+            grouped = grouped_w1[a]
             halves = len(w1_raw[a])
             for u, part in enumerate(w1_raw[a]):
                 m_cols = slice(u * P // halves, (u + 1) * P // halves)
@@ -182,8 +149,46 @@ def tile_list_crease_bridge_features_kernel(
             w1_codes.append(codes)
             w1_scale.append(scales)
 
+        prepare_pass(0)
+        w1_raw.append(load_w1(2, ["grouped0", "chain_c"]))
+
+        depth_first = keep.tile([P, 2 * S + 32], F32, name="depth_first", tag="chain_a", align_bytes=64)
+        depth_second = keep.tile([P, 2, S], F32, name="depth_second", tag="grouped0", align_bytes=64)
+        depth_sb = [depth_first[:, 0:S], depth_first[:, S : 2 * S], depth_second[:, 0, :], depth_second[:, 1, :]]
+        wear_wgs = keep.tile([P, 2, PACK, PICK], F32, name="wear_wgs", tag="chain_b", align_bytes=64)
+        wear_sb = wear_wgs[:, 0, :, :]
+        wgs_sb = wear_wgs[:, 1, :, :]
+        nc.sync.dma_start(out=depth_sb[0], in_=by_row(depth)[:, 0, :])
+        for n, (name, vec) in enumerate((("slope", slope), ("share", share), ("skip", skip), ("gain", gain))):
+            row_values[name] = depth_first[:, 2 * S + 8 * n : 2 * S + 8 * n + PACK]
+            nc.sync.dma_start(out=row_values[name], in_=vec.rearrange("(p i) -> p i", i=PACK))
+        nc.sync.dma_start(out=depth_sb[1], in_=by_row(depth)[:, 1, :])
+        nc.sync.dma_start(out=wear_sb[:, 0, :], in_=by_row(wear)[:, 0, :])
+        for q in (0, 2, 1, 3):
+            nc.sync.dma_start(out=wgs_sb[32 * q : 32 * q + 32, :, :], in_=by_row(wgs))
+        nc.sync.dma_start(out=depth_sb[2], in_=by_row(depth)[:, 2, :])
+        nc.sync.dma_start(out=wear_sb[:, 1:PACK, :], in_=by_row(wear)[:, 1:PACK, :])
+        nc.sync.dma_start(out=depth_sb[3], in_=by_row(depth)[:, 3, :])
+
+        prepare_pass(1)
+        prepare_pass(2)
+        open_at = keep.tile([P, PACK], F32, name="open_at")
+        nc.vector.scalar_tensor_tensor(
+            out=open_at[:], in0=row_values["slope"], scalar=-1.0, in1=row_values["share"],
+            op0=ALU.mult, op1=ALU.mult,
+        )
+
+        w3_scale_raw = keep.tile([P, H], U8, name="w3_scale_raw", tag="grouped1", align_bytes=64)
+        nc.gpsimd.memset(w3_scale_raw[:].bitcast(I32), 0)
+        for r in range(4):
+            nc.sync.dma_start(out=w3_scale_raw[r:P:32, :].bitcast(I32), in_=w3_scales[0, r:16:4, :].bitcast(I32))
+        w3_raw = keep.tile([P, H], U32, name="w3_raw", tag="grouped2", align_bytes=64)
+        nc.sync.dma_start(out=w3_raw[:].bitcast(I32), in_=w3_words[0].rearrange("p c i -> p (c i)").bitcast(I32))
+        room_sb = keep.tile([P, PACK, S], F32, name="room_sb", tag="chain_c", align_bytes=64)
+        nc.sync.dma_start(out=room_sb[:], in_=by_row(room))
+
         h = [keep.tile([P, S], F32, name="h%d" % i) for i in range(PACK)]
-        top = keep.tile([P, PACK], F32, name="top")
+        top = keep.tile([P, PACK, S // BANK], F32, name="top")
         look_bias = keep.tile([P, PACK], F32, name="look_bias")
         page_grouped = [
             keep.tile([P, width, PACK], BF16, name="page_grouped%d" % n, align_bytes=64)
@@ -211,18 +216,24 @@ def tile_list_crease_bridge_features_kernel(
                         lhsT_scale=w1_scale[a][:, cols], rhs=v_codes[a][:, j_cols].bitcast(FP8X4),
                         rhs_scale=v_scales[:, a, j_cols], start=(a == 0), stop=(a == PASSES - 1),
                     )
-            deep = [ring.tile([P, BANK], F32, name="deep%d_%d" % (i, c), tag="deep") for c in halves]
+            deep = [
+                keep.tile([P, BANK], F32, name="deep%d_%d" % (i, c), tag="turn%d" % (i - 1 + c)) for c in halves
+            ]
             for c in halves:
                 nc.vector.tensor_tensor(
-                    out=deep[c][:], in0=by_w1[c][:], in1=depth_sb[:, i, c * BANK : (c + 1) * BANK], op=ALU.mult
+                    out=deep[c][:], in0=by_w1[c][:], in1=depth_sb[i][:, c * BANK : (c + 1) * BANK], op=ALU.mult
                 )
             for c in halves:
                 nc.vector.tensor_tensor(
                     out=h[i][:, c * BANK : (c + 1) * BANK], in0=by_w4[c][:], in1=deep[c][:], op=ALU.max
                 )
-            nc.vector.reduce_max(out=top[:, i : i + 1], in_=h[i][:], axis=AXIS.X)
-            nc.scalar.activation(
-                out=look_bias[:, i : i + 1], in_=top[:, i : i + 1], func=ACT.Copy, scale=open_at[:, i : i + 1]
+            for c in halves:
+                nc.vector.reduce_max(
+                    out=top[:, i, c : c + 1], in_=h[i][:, c * BANK : (c + 1) * BANK], axis=AXIS.X
+                )
+            nc.vector.tensor_scalar(
+                out=look_bias[:, i : i + 1], in0=top[:, i, 0:1], scalar1=top[:, i, 1:2],
+                scalar2=open_at[:, i : i + 1], op0=ALU.max, op1=ALU.mult,
             )
             looks[i] = ring.tile([P, PICK], F32, name="look%d" % i, tag="look")
             nc.scalar.activation(
@@ -235,9 +246,8 @@ def tile_list_crease_bridge_features_kernel(
             )
 
         def rewrite(i):
-            worn = ring.tile([P, PICK], F32, name="worn%d" % i, tag="worn")
-            engine = nc.vector
-            engine.tensor_tensor(out=worn[:], in0=looks[i][:], in1=wear_sb[:, i, :], op=ALU.subtract)
+            worn = keep.tile([P, PICK], F32, name="worn%d" % i, tag="turn%d" % (i + 1))
+            nc.vector.tensor_tensor(out=worn[:], in0=looks[i][:], in1=wear_sb[:, i, :], op=ALU.subtract)
             nc.vector.tensor_tensor(
                 out=pages[i][:].indirect(pos2_sb[:]), in0=worn[:], in1=wgs_sb[:, i, :], op=ALU.mult
             )
@@ -250,13 +260,18 @@ def tile_list_crease_bridge_features_kernel(
         features(0)
         for i in range(1, PACK):
             features(i)
-            if i == 1:
+            if i == 2:
                 nc.scalar.copy(
                     out=w3_codes[:].rearrange("p (i m) -> p i m", i=PACK),
                     in_=w3_raw[:].rearrange("p (m i) -> p i m", i=PACK),
                 )
             rewrite(i - 1)
         rewrite(PACK - 1)
+
+        nc.vector.tensor_copy(
+            out=w3_scale[:].rearrange("p (i m) -> p i m", i=PACK),
+            in_=w3_scale_raw[:].rearrange("p (m i) -> p i m", i=PACK),
+        )
 
         def read_out_products(n, first_bank, tag):
             start, width = READ_OUT[n]
@@ -280,28 +295,29 @@ def tile_list_crease_bridge_features_kernel(
                 sums.append(place)
             return sums
 
+        scaled = keep.tile([P, PACK, S], F32, name="scaled")
+
         def times_h(n, sums):
             start, width = READ_OUT[n]
-            scaled = keep.tile([P, PACK, width], F32, name="scaled%d" % n, tag="scaled%d" % n, align_bytes=64)
             for i in range(PACK):
                 nc.vector.tensor_tensor(
-                    out=scaled[:, i, :], in0=sums[i], in1=h[i][:, start : start + width], op=ALU.mult
+                    out=scaled[:, i, start : start + width], in0=sums[i], in1=h[i][:, start : start + width],
+                    op=ALU.mult,
                 )
-            return scaled
 
-        def plus_room(n, scaled, rows, engine):
-            start, width = READ_OUT[n]
-            place = room_sb[:, rows, start : start + width]
-            engine.tensor_tensor(out=place, in0=scaled[:, rows, :], in1=place, op=ALU.add)
-            nc.sync.dma_start(out=by_row(out)[:, rows, start : start + width], in_=place)
+        def plus_room(half, i, engine):
+            cols = slice(half * BANK, (half + 1) * BANK)
+            engine.tensor_tensor(out=room_sb[:, i, cols], in0=scaled[:, i, cols], in1=room_sb[:, i, cols], op=ALU.add)
+            nc.sync.dma_start(out=by_row(out)[:, i, cols], in_=room_sb[:, i, cols])
 
         sums0 = read_out_products(0, 0, "codes0")
         sums1 = read_out_products(1, 2, "codes1")
-        scaled0 = times_h(0, sums0)
-        plus_room(0, scaled0, slice(0, PACK), nc.vector)
-        sums2 = read_out_products(2, 4, "scaled0")
-        scaled1 = times_h(1, sums1)
-        plus_room(1, scaled1, slice(0, PACK), nc.vector)
-        scaled2 = times_h(2, sums2)
+        times_h(0, sums0)
+        sums2 = read_out_products(2, 4, "codes0")
+        times_h(1, sums1)
+        for i in range(PACK - 1):
+            plus_room(0, i, nc.gpsimd)
+        times_h(2, sums2)
+        plus_room(0, PACK - 1, nc.vector)
         for i in range(PACK):
-            plus_room(2, scaled2, slice(i, i + 1), nc.vector)
+            plus_room(1, i, nc.vector)

@@ -34,6 +34,7 @@ def tile_list_crease_bridge_features_kernel(
         lists = ctx.enter_context(tc.tile_pool(name="lists", bufs=1))
         keep = ctx.enter_context(tc.tile_pool(name="keep", bufs=1))
         ring = ctx.enter_context(tc.tile_pool(name="ring", bufs=2))
+        turns = ctx.enter_context(tc.tile_pool(name="turns", bufs=1))
         psum = ctx.enter_context(tc.psum_pool(name="psum", bufs=1))
 
         def bank(n, name):
@@ -111,7 +112,6 @@ def tile_list_crease_bridge_features_kernel(
         w4_codes = keep.tile([P, PASSES, 2 * H], U8, name="w4_codes", align_bytes=64)
         w4_scale = keep.tile([P, PASSES, H], U8, name="w4_scale", align_bytes=64)
         w3_codes = keep.tile([P, H], U32, name="w3_codes", align_bytes=64)
-        w3_scale = keep.tile([P, H], U8, name="w3_scale", align_bytes=64)
         nc.vector.tensor_copy(
             out=w4_codes[:].bitcast(U16).rearrange("p a (i m) -> p a i m", i=PACK),
             in_=w4_raw[:].bitcast(U16).rearrange("p a (m i) -> p a i m", i=PACK),
@@ -163,12 +163,14 @@ def tile_list_crease_bridge_features_kernel(
             row_values[name] = depth_first[:, 2 * S + 8 * n : 2 * S + 8 * n + PACK]
             nc.sync.dma_start(out=row_values[name], in_=vec.rearrange("(p i) -> p i", i=PACK))
         nc.sync.dma_start(out=depth_sb[1], in_=by_row(depth)[:, 1, :])
+        nc.sync.dma_start(out=depth_sb[2], in_=by_row(depth)[:, 2, :])
         nc.sync.dma_start(out=wear_sb[:, 0, :], in_=by_row(wear)[:, 0, :])
         for q in (0, 2, 1, 3):
-            nc.sync.dma_start(out=wgs_sb[32 * q : 32 * q + 32, :, :], in_=by_row(wgs))
-        nc.sync.dma_start(out=depth_sb[2], in_=by_row(depth)[:, 2, :])
-        nc.sync.dma_start(out=wear_sb[:, 1:PACK, :], in_=by_row(wear)[:, 1:PACK, :])
+            nc.sync.dma_start(out=wgs_sb[32 * q : 32 * q + 32, 0, :], in_=by_row(wgs)[:, 0, :])
         nc.sync.dma_start(out=depth_sb[3], in_=by_row(depth)[:, 3, :])
+        for q in (0, 2, 1, 3):
+            nc.sync.dma_start(out=wgs_sb[32 * q : 32 * q + 32, 1:PACK, :], in_=by_row(wgs)[:, 1:PACK, :])
+        nc.sync.dma_start(out=wear_sb[:, 1:PACK, :], in_=by_row(wear)[:, 1:PACK, :])
 
         prepare_pass(1)
         prepare_pass(2)
@@ -187,7 +189,18 @@ def tile_list_crease_bridge_features_kernel(
         room_sb = keep.tile([P, PACK, S], F32, name="room_sb", tag="chain_c", align_bytes=64)
         nc.sync.dma_start(out=room_sb[:], in_=by_row(room))
 
-        h = [keep.tile([P, S], F32, name="h%d" % i) for i in range(PACK)]
+        KIB = 1024
+        h_place = [None, None, 0, 8 * KIB]
+        deep_place = [None, 2 * KIB, 10 * KIB, 4 * KIB]
+        worn_place = [3 * KIB, 11 * KIB, 6 * KIB, None]
+
+        def placed(shape, name, place):
+            if place is None:
+                return keep.tile(shape, F32, name=name)
+            return turns.tile(shape, F32, name=name, offset=place)
+
+        h = [placed([P, S], "h%d" % i, h_place[i]) for i in range(PACK)]
+        deep = [placed([P, S], "deep%d" % i, deep_place[i]) for i in range(PACK)]
         top = keep.tile([P, PACK, S // BANK], F32, name="top")
         look_bias = keep.tile([P, PACK], F32, name="look_bias")
         page_grouped = [
@@ -196,37 +209,39 @@ def tile_list_crease_bridge_features_kernel(
         ]
         looks, pages = {}, {}
 
-        def features(i):
+        halves = range(S // BANK)
+
+        def product(i, first_bank, by_w1):
             cols = slice(i * P, (i + 1) * P)
-            halves = range(S // BANK)
-            by_w1 = [bank(4 * (i % 2) + c, "by_w1_%d_%d" % (i, c)) for c in halves]
-            by_w4 = [bank(4 * (i % 2) + 2 + c, "by_w4_%d_%d" % (i, c)) for c in halves]
+            sums = [bank(first_bank + c, "sum%d_%d_%d" % (by_w1, i, c)) for c in halves]
             for a in range(PASSES):
+                if by_w1:
+                    codes, scales = w1_codes[a][:, cols].bitcast(FP8X4), w1_scale[a][:, cols]
+                else:
+                    codes, scales = w4_codes[:, a, 2 * i * P : 2 * (i + 1) * P].bitcast(FP4X4), w4_scale[:, a, cols]
                 for c in halves:
                     j_cols = slice(c * BANK, (c + 1) * BANK)
                     nc.tensor.matmul_mx(
-                        out=by_w4[c][:], lhsT=w4_codes[:, a, 2 * i * P : 2 * (i + 1) * P].bitcast(FP4X4),
-                        lhsT_scale=w4_scale[:, a, cols], rhs=v_codes[a][:, j_cols].bitcast(FP8X4),
+                        out=sums[c][:], lhsT=codes, lhsT_scale=scales, rhs=v_codes[a][:, j_cols].bitcast(FP8X4),
                         rhs_scale=v_scales[:, a, j_cols], start=(a == 0), stop=(a == PASSES - 1),
                     )
-                for c in halves:
-                    j_cols = slice(c * BANK, (c + 1) * BANK)
-                    nc.tensor.matmul_mx(
-                        out=by_w1[c][:], lhsT=w1_codes[a][:, cols].bitcast(FP8X4),
-                        lhsT_scale=w1_scale[a][:, cols], rhs=v_codes[a][:, j_cols].bitcast(FP8X4),
-                        rhs_scale=v_scales[:, a, j_cols], start=(a == 0), stop=(a == PASSES - 1),
-                    )
-            deep = [
-                keep.tile([P, BANK], F32, name="deep%d_%d" % (i, c), tag="turn%d" % (i - 1 + c)) for c in halves
-            ]
+            return sums
+
+        def bring_out(i, sums):
+            copied = keep.tile([P, S], F32, name="by_w1_%d" % i)
             for c in halves:
-                nc.vector.tensor_tensor(
-                    out=deep[c][:], in0=by_w1[c][:], in1=depth_sb[i][:, c * BANK : (c + 1) * BANK], op=ALU.mult
-                )
+                nc.scalar.copy(out=copied[:, c * BANK : (c + 1) * BANK], in_=sums[c][:])
+            return [copied[:, c * BANK : (c + 1) * BANK] for c in halves]
+
+        def times_depth(i, sums, engine):
             for c in halves:
-                nc.vector.tensor_tensor(
-                    out=h[i][:, c * BANK : (c + 1) * BANK], in0=by_w4[c][:], in1=deep[c][:], op=ALU.max
-                )
+                cols = slice(c * BANK, (c + 1) * BANK)
+                engine.tensor_tensor(out=deep[i][:, cols], in0=sums[c], in1=depth_sb[i][:, cols], op=ALU.mult)
+
+        def features(i, by_w4):
+            for c in halves:
+                cols = slice(c * BANK, (c + 1) * BANK)
+                nc.vector.tensor_tensor(out=h[i][:, cols], in0=by_w4[c][:], in1=deep[i][:, cols], op=ALU.max)
             for c in halves:
                 nc.vector.reduce_max(
                     out=top[:, i, c : c + 1], in_=h[i][:, c * BANK : (c + 1) * BANK], axis=AXIS.X
@@ -246,7 +261,7 @@ def tile_list_crease_bridge_features_kernel(
             )
 
         def rewrite(i):
-            worn = keep.tile([P, PICK], F32, name="worn%d" % i, tag="turn%d" % (i + 1))
+            worn = placed([P, PICK], "worn%d" % i, worn_place[i])
             nc.vector.tensor_tensor(out=worn[:], in0=looks[i][:], in1=wear_sb[:, i, :], op=ALU.subtract)
             nc.vector.tensor_tensor(
                 out=pages[i][:].indirect(pos2_sb[:]), in0=worn[:], in1=wgs_sb[:, i, :], op=ALU.mult
@@ -257,21 +272,33 @@ def tile_list_crease_bridge_features_kernel(
                     scale=row_values["gain"][:, i : i + 1],
                 )
 
-        features(0)
-        for i in range(1, PACK):
-            features(i)
-            if i == 2:
-                nc.scalar.copy(
-                    out=w3_codes[:].rearrange("p (i m) -> p i m", i=PACK),
-                    in_=w3_raw[:].rearrange("p (m i) -> p i m", i=PACK),
-                )
-            rewrite(i - 1)
-        rewrite(PACK - 1)
-
-        nc.vector.tensor_copy(
+        by_w1 = [product(i, 2 * i, True) for i in range(3)]
+        by_w4 = [product(0, 6, False)]
+        times_depth(0, [acc[:] for acc in by_w1[0]], nc.vector)
+        for i in (1, 2):
+            times_depth(i, bring_out(i, by_w1[i]), nc.gpsimd)
+        by_w4.append(product(1, 0, False))
+        features(0, by_w4[0])
+        last_by_w1 = bring_out(3, product(3, 4, True))
+        by_w4.append(product(2, 2, False))
+        by_w4.append(product(3, 6, False))
+        features(1, by_w4[1])
+        rewrite(0)
+        times_depth(3, last_by_w1, nc.gpsimd)
+        features(2, by_w4[2])
+        nc.scalar.copy(
+            out=w3_codes[:].rearrange("p (i m) -> p i m", i=PACK),
+            in_=w3_raw[:].rearrange("p (m i) -> p i m", i=PACK),
+        )
+        rewrite(1)
+        w3_scale = turns.tile([P, H], U8, name="w3_scale", offset=12 * KIB, align_bytes=64)
+        nc.gpsimd.tensor_copy(
             out=w3_scale[:].rearrange("p (i m) -> p i m", i=PACK),
             in_=w3_scale_raw[:].rearrange("p (m i) -> p i m", i=PACK),
         )
+        features(3, by_w4[3])
+        rewrite(2)
+        rewrite(3)
 
         def read_out_products(n, first_bank, tag):
             start, width = READ_OUT[n]
@@ -305,8 +332,8 @@ def tile_list_crease_bridge_features_kernel(
                     op=ALU.mult,
                 )
 
-        def plus_room(half, i, engine):
-            cols = slice(half * BANK, (half + 1) * BANK)
+        def plus_room(start, width, i, engine):
+            cols = slice(start, start + width)
             engine.tensor_tensor(out=room_sb[:, i, cols], in0=scaled[:, i, cols], in1=room_sb[:, i, cols], op=ALU.add)
             nc.sync.dma_start(out=by_row(out)[:, i, cols], in_=room_sb[:, i, cols])
 
@@ -316,8 +343,8 @@ def tile_list_crease_bridge_features_kernel(
         sums2 = read_out_products(2, 4, "codes0")
         times_h(1, sums1)
         for i in range(PACK - 1):
-            plus_room(0, i, nc.gpsimd)
+            plus_room(0, BANK, i, nc.gpsimd)
         times_h(2, sums2)
-        plus_room(0, PACK - 1, nc.vector)
+        plus_room(0, BANK, PACK - 1, nc.vector)
         for i in range(PACK):
-            plus_room(1, i, nc.vector)
+            plus_room(BANK, BANK, i, nc.vector)

@@ -1,6 +1,7 @@
 from contextlib import ExitStack
 
 import concourse.mybir as mybir
+from concourse.masks import make_identity
 
 K, T, S, PICK, H = 1536, 4096, 1024, 512, 512
 FLOPS = 2 * 2 * K * H * S + 2 * H * H * S
@@ -20,9 +21,20 @@ AXIS = mybir.AxisListType
 P = 128
 PACK = 4
 PASSES = K // (P * PACK)
-QUADS = 4
+BLOCKS = 16
+QUAD = 32
+SCALE_ROWS = 4
+QUAD_ORDER = (0, 2, 1, 3)
+LIST_ROWS = 16
 BANK = 512
+KIB = 1024
+TAB0_PIECES = 4
+VECTOR_PITCH = 8
 READ_OUT = ((0, 256), (256, 256), (512, 512))
+H_OFFSET = (None, None, 0, 8 * KIB)
+DEEP_OFFSET = (None, 2 * KIB, 10 * KIB, 4 * KIB)
+WORN_OFFSET = (3 * KIB, 11 * KIB, 6 * KIB, None)
+W3_SCALE_OFFSET = 12 * KIB
 
 
 def tile_list_crease_bridge_features_kernel(
@@ -37,8 +49,8 @@ def tile_list_crease_bridge_features_kernel(
         turns = ctx.enter_context(tc.tile_pool(name="turns", bufs=1))
         psum = ctx.enter_context(tc.psum_pool(name="psum", bufs=1))
 
-        def bank(n, name):
-            return psum.tile([P, BANK], F32, name=name, tag="bank%d" % n)
+        def bank(number, name):
+            return psum.tile([P, BANK], F32, name=name, tag="bank%d" % number)
 
         def by_row(matrix):
             return matrix.rearrange("(p i) c -> p i c", i=PACK)
@@ -50,14 +62,16 @@ def tile_list_crease_bridge_features_kernel(
         nc.gpsimd.memset(w4_scale_raw[:].bitcast(I32), 0)
         nc.vector.memset(v_scales[:].bitcast(I32), 0)
 
-        offs_sb = lists.tile([P, S // 16], U16, name="offs_sb")
-        pos1_sb = lists.tile([P, PICK // 16], U16, name="pos1_sb")
-        pos2_sb = lists.tile([P, PICK // 16], U16, name="pos2_sb")
-        row_values = {}
+        identity = keep.tile([P, P], F32, name="identity")
+        make_identity(nc, identity[:])
+
+        offs_sb = lists.tile([P, S // LIST_ROWS], U16, name="offs_sb")
+        pos1_sb = lists.tile([P, PICK // LIST_ROWS], U16, name="pos1_sb")
+        pos2_sb = lists.tile([P, PICK // LIST_ROWS], U16, name="pos2_sb")
 
         def load_tab(a, tag):
             words = keep.tile([P, T], U32, name="tab%d" % a, tag=tag, align_bytes=64)
-            nc.sync.dma_start(out=words[:].bitcast(I32), in_=tab_words[a].rearrange("p t i -> p (t i)").bitcast(I32))
+            nc.sync.dma_start(out=words[:].bitcast(I32), in_=tab_words[a].rearrange("p t j -> p (t j)").bitcast(I32))
             return words
 
         def load_w1(a, tags):
@@ -71,9 +85,9 @@ def tile_list_crease_bridge_features_kernel(
             return parts
 
         tab = [keep.tile([P, T], U32, name="tab0", align_bytes=64)]
-        tab0_words = tab_words[0].rearrange("p t i -> p (t i)").bitcast(I32)
-        for u in range(4):
-            cols = slice(u * T // 4, (u + 1) * T // 4)
+        tab0_words = tab_words[0].rearrange("p t j -> p (t j)").bitcast(I32)
+        for u in range(TAB0_PIECES):
+            cols = slice(u * T // TAB0_PIECES, (u + 1) * T // TAB0_PIECES)
             nc.sync.dma_start(out=tab[0][:, cols].bitcast(I32), in_=tab0_words[:, cols])
             if u == 0:
                 nc.sync.dma_start(offs_sb[:], offs)
@@ -81,30 +95,29 @@ def tile_list_crease_bridge_features_kernel(
         nc.sync.dma_start(out=w4_raw[:].bitcast(I32), in_=w4_words.rearrange("a p c -> p a c").bitcast(I32))
         nc.sync.dma_start(pos1_sb[:], pos1)
         nc.sync.dma_start(pos2_sb[:], pos2)
-        live_rows = PASSES * 16
         nc.sync.dma_start(
-            out=tab_scale_rows[0 : 2 * live_rows : 2, :].bitcast(I32),
+            out=tab_scale_rows[0 : 2 * PASSES * BLOCKS : 2, :].bitcast(I32),
             in_=tab_scales.rearrange("a q t -> q a t").bitcast(I32),
         )
         w1_raw = [load_w1(0, ["w1_raw0"])]
-        for r in range(4):
+        for r in range(SCALE_ROWS):
             nc.sync.dma_start(
-                out=w4_scale_raw[r:P:32, :, :].bitcast(I32),
-                in_=w4_scales[:, r:16:4, :].rearrange("a q c -> q a c").bitcast(I32),
+                out=w4_scale_raw[r:P:QUAD, :, :].bitcast(I32),
+                in_=w4_scales[:, r:BLOCKS:SCALE_ROWS, :].rearrange("a q c -> q a c").bitcast(I32),
             )
         tab.append(load_tab(1, "chain_c"))
 
         picked_scale_rows = keep.tile([P, S], U8, name="picked_scale_rows")
         nc.vector.tensor_copy(out=picked_scale_rows[:], in_=tab_scale_rows[:].indirect(offs_sb[:]))
         w1_raw.append(load_w1(1, ["chain_a"]))
-        rows_a_quad = 4 * PASSES
-        for q in (0, 2, 1, 3):
+        span = 2 * SCALE_ROWS * PASSES
+        for quad in QUAD_ORDER:
             nc.sync.dma_start(
-                out=v_scales[32 * q : 32 * q + 4, :, :].bitcast(I32),
-                in_=picked_scale_rows[2 * rows_a_quad * q : 2 * rows_a_quad * (q + 1) : 2, :].bitcast(I32),
+                out=v_scales[QUAD * quad : QUAD * quad + SCALE_ROWS, :, :].bitcast(I32),
+                in_=picked_scale_rows[span * quad : span * (quad + 1) : 2, :].bitcast(I32),
             )
         tab.append(load_tab(2, "chain_b"))
-        grouped_w1 = [
+        w1_grouped = [
             keep.tile([P, PACK, P, PACK], BF16, name="w1_grouped%d" % a, tag="grouped%d" % a, align_bytes=64)
             for a in range(PASSES)
         ]
@@ -128,23 +141,25 @@ def tile_list_crease_bridge_features_kernel(
             nc.vector.tensor_copy(out=picked[:], in_=tab[a][:].indirect(offs_sb[:]))
             v_codes.append(picked)
 
-            grouped = grouped_w1[a]
-            halves = len(w1_raw[a])
+            grouped = w1_grouped[a]
+            n_parts = len(w1_raw[a])
             for u, part in enumerate(w1_raw[a]):
-                m_cols = slice(u * P // halves, (u + 1) * P // halves)
-                copy = nc.scalar.copy if u == 0 else nc.vector.tensor_copy
-                copy(
-                    out=grouped[:, :, m_cols, :].rearrange("p i m j -> p m j i"),
-                    in_=part[:].rearrange("p j (m i) -> p m j i", i=PACK),
-                )
+                m_cols = slice(u * P // n_parts, (u + 1) * P // n_parts)
+                dealt = grouped[:, :, m_cols, :].rearrange("p i m j -> p m j i")
+                source = part[:].rearrange("p j (m i) -> p m j i", i=PACK)
+                if u == 0:
+                    nc.scalar.copy(out=dealt, in_=source)
+                else:
+                    nc.vector.tensor_copy(out=dealt[:, :, :, 0], in_=source[:, :, :, 0])
+                    nc.scalar.copy(out=dealt[:, :, :, 1:PACK], in_=source[:, :, :, 1:PACK])
             codes = keep.tile([P, H], U32, name="w1_codes%d" % a, align_bytes=64)
             scales = keep.tile([P, H], U8, name="w1_scale%d" % a, align_bytes=64)
-            step = PACK if a < PASSES - 1 else 1
-            for i in range(0, PACK, step):
-                cols = slice(i * P, (i + step) * P)
+            sets_at_once = PACK if a < PASSES - 1 else 1
+            for i in range(0, PACK, sets_at_once):
+                cols = slice(i * P, (i + sets_at_once) * P)
                 nc.vector.quantize_mx(
                     out=codes[:, cols].bitcast(FP8X4), scales=scales[:, cols],
-                    in_=grouped[:, i : i + step, :, :].rearrange("p i m j -> p (i m j)"),
+                    in_=grouped[:, i : i + sets_at_once, :, :].rearrange("p i m j -> p (i m j)"),
                 )
             w1_codes.append(codes)
             w1_scale.append(scales)
@@ -152,55 +167,57 @@ def tile_list_crease_bridge_features_kernel(
         prepare_pass(0)
         w1_raw.append(load_w1(2, ["grouped0", "chain_c"]))
 
-        depth_first = keep.tile([P, 2 * S + 32], F32, name="depth_first", tag="chain_a", align_bytes=64)
+        vectors = (("slope", slope), ("share", share), ("skip", skip), ("gain", gain))
+        depth_first = keep.tile(
+            [P, 2 * S + len(vectors) * VECTOR_PITCH], F32, name="depth_first", tag="chain_a", align_bytes=64
+        )
         depth_second = keep.tile([P, 2, S], F32, name="depth_second", tag="grouped0", align_bytes=64)
         depth_sb = [depth_first[:, 0:S], depth_first[:, S : 2 * S], depth_second[:, 0, :], depth_second[:, 1, :]]
         wear_wgs = keep.tile([P, 2, PACK, PICK], F32, name="wear_wgs", tag="chain_b", align_bytes=64)
         wear_sb = wear_wgs[:, 0, :, :]
         wgs_sb = wear_wgs[:, 1, :, :]
         nc.sync.dma_start(out=depth_sb[0], in_=by_row(depth)[:, 0, :])
-        for n, (name, vec) in enumerate((("slope", slope), ("share", share), ("skip", skip), ("gain", gain))):
-            row_values[name] = depth_first[:, 2 * S + 8 * n : 2 * S + 8 * n + PACK]
-            nc.sync.dma_start(out=row_values[name], in_=vec.rearrange("(p i) -> p i", i=PACK))
+        row_values = {}
+        for number, (name, vector) in enumerate(vectors):
+            first = 2 * S + VECTOR_PITCH * number
+            row_values[name] = depth_first[:, first : first + PACK]
+            nc.sync.dma_start(out=row_values[name], in_=vector.rearrange("(p i) -> p i", i=PACK))
         nc.sync.dma_start(out=depth_sb[1], in_=by_row(depth)[:, 1, :])
         nc.sync.dma_start(out=depth_sb[2], in_=by_row(depth)[:, 2, :])
         nc.sync.dma_start(out=wear_sb[:, 0, :], in_=by_row(wear)[:, 0, :])
-        for q in (0, 2, 1, 3):
-            nc.sync.dma_start(out=wgs_sb[32 * q : 32 * q + 32, 0, :], in_=by_row(wgs)[:, 0, :])
+        for quad in QUAD_ORDER:
+            nc.sync.dma_start(out=wgs_sb[QUAD * quad : QUAD * (quad + 1), 0, :], in_=by_row(wgs)[:, 0, :])
         nc.sync.dma_start(out=depth_sb[3], in_=by_row(depth)[:, 3, :])
-        for q in (0, 2, 1, 3):
-            nc.sync.dma_start(out=wgs_sb[32 * q : 32 * q + 32, 1:PACK, :], in_=by_row(wgs)[:, 1:PACK, :])
+        for quad in QUAD_ORDER:
+            nc.sync.dma_start(out=wgs_sb[QUAD * quad : QUAD * (quad + 1), 1:PACK, :], in_=by_row(wgs)[:, 1:PACK, :])
         nc.sync.dma_start(out=wear_sb[:, 1:PACK, :], in_=by_row(wear)[:, 1:PACK, :])
 
         prepare_pass(1)
         prepare_pass(2)
-        open_at = keep.tile([P, PACK], F32, name="open_at")
+        top_factor = keep.tile([P, PACK], F32, name="top_factor")
         nc.vector.scalar_tensor_tensor(
-            out=open_at[:], in0=row_values["slope"], scalar=-1.0, in1=row_values["share"],
+            out=top_factor[:], in0=row_values["slope"], scalar=-1.0, in1=row_values["share"],
             op0=ALU.mult, op1=ALU.mult,
         )
 
         w3_scale_raw = keep.tile([P, H], U8, name="w3_scale_raw", tag="grouped1", align_bytes=64)
         nc.gpsimd.memset(w3_scale_raw[:].bitcast(I32), 0)
-        for r in range(4):
-            nc.sync.dma_start(out=w3_scale_raw[r:P:32, :].bitcast(I32), in_=w3_scales[0, r:16:4, :].bitcast(I32))
+        for r in range(SCALE_ROWS):
+            nc.sync.dma_start(
+                out=w3_scale_raw[r:P:QUAD, :].bitcast(I32), in_=w3_scales[0, r:BLOCKS:SCALE_ROWS, :].bitcast(I32)
+            )
         w3_raw = keep.tile([P, H], U32, name="w3_raw", tag="grouped2", align_bytes=64)
-        nc.sync.dma_start(out=w3_raw[:].bitcast(I32), in_=w3_words[0].rearrange("p c i -> p (c i)").bitcast(I32))
+        nc.sync.dma_start(out=w3_raw[:].bitcast(I32), in_=w3_words[0].rearrange("p c j -> p (c j)").bitcast(I32))
         room_sb = keep.tile([P, PACK, S], F32, name="room_sb", tag="chain_c", align_bytes=64)
         nc.sync.dma_start(out=room_sb[:], in_=by_row(room))
 
-        KIB = 1024
-        h_place = [None, None, 0, 8 * KIB]
-        deep_place = [None, 2 * KIB, 10 * KIB, 4 * KIB]
-        worn_place = [3 * KIB, 11 * KIB, 6 * KIB, None]
-
-        def placed(shape, name, place):
-            if place is None:
+        def placed(shape, name, offset):
+            if offset is None:
                 return keep.tile(shape, F32, name=name)
-            return turns.tile(shape, F32, name=name, offset=place)
+            return turns.tile(shape, F32, name=name, offset=offset)
 
-        h = [placed([P, S], "h%d" % i, h_place[i]) for i in range(PACK)]
-        deep = [placed([P, S], "deep%d" % i, deep_place[i]) for i in range(PACK)]
+        h = [placed([P, S], "h%d" % i, H_OFFSET[i]) for i in range(PACK)]
+        deep = [placed([P, S], "deep%d" % i, DEEP_OFFSET[i]) for i in range(PACK)]
         top = keep.tile([P, PACK, S // BANK], F32, name="top")
         look_bias = keep.tile([P, PACK], F32, name="look_bias")
         page_grouped = [
@@ -211,11 +228,11 @@ def tile_list_crease_bridge_features_kernel(
 
         halves = range(S // BANK)
 
-        def product(i, first_bank, by_w1):
+        def product(i, first_bank, of_w1):
             cols = slice(i * P, (i + 1) * P)
-            sums = [bank(first_bank + c, "sum%d_%d_%d" % (by_w1, i, c)) for c in halves]
+            sums = [bank(first_bank + c, "sum%d_%d_%d" % (of_w1, i, c)) for c in halves]
             for a in range(PASSES):
-                if by_w1:
+                if of_w1:
                     codes, scales = w1_codes[a][:, cols].bitcast(FP8X4), w1_scale[a][:, cols]
                 else:
                     codes, scales = w4_codes[:, a, 2 * i * P : 2 * (i + 1) * P].bitcast(FP4X4), w4_scale[:, a, cols]
@@ -228,7 +245,7 @@ def tile_list_crease_bridge_features_kernel(
             return sums
 
         def bring_out(i, sums):
-            copied = keep.tile([P, S], F32, name="by_w1_%d" % i)
+            copied = keep.tile([P, S], F32, name="w1_sums%d" % i)
             for c in halves:
                 nc.scalar.copy(out=copied[:, c * BANK : (c + 1) * BANK], in_=sums[c][:])
             return [copied[:, c * BANK : (c + 1) * BANK] for c in halves]
@@ -238,17 +255,17 @@ def tile_list_crease_bridge_features_kernel(
                 cols = slice(c * BANK, (c + 1) * BANK)
                 engine.tensor_tensor(out=deep[i][:, cols], in0=sums[c], in1=depth_sb[i][:, cols], op=ALU.mult)
 
-        def features(i, by_w4):
+        def features(i, w4_sums):
             for c in halves:
                 cols = slice(c * BANK, (c + 1) * BANK)
-                nc.vector.tensor_tensor(out=h[i][:, cols], in0=by_w4[c][:], in1=deep[i][:, cols], op=ALU.max)
+                nc.vector.tensor_tensor(out=h[i][:, cols], in0=w4_sums[c][:], in1=deep[i][:, cols], op=ALU.max)
             for c in halves:
                 nc.vector.reduce_max(
                     out=top[:, i, c : c + 1], in_=h[i][:, c * BANK : (c + 1) * BANK], axis=AXIS.X
                 )
             nc.vector.tensor_scalar(
                 out=look_bias[:, i : i + 1], in0=top[:, i, 0:1], scalar1=top[:, i, 1:2],
-                scalar2=open_at[:, i : i + 1], op0=ALU.max, op1=ALU.mult,
+                scalar2=top_factor[:, i : i + 1], op0=ALU.max, op1=ALU.mult,
             )
             looks[i] = ring.tile([P, PICK], F32, name="look%d" % i, tag="look")
             nc.scalar.activation(
@@ -261,7 +278,7 @@ def tile_list_crease_bridge_features_kernel(
             )
 
         def rewrite(i):
-            worn = placed([P, PICK], "worn%d" % i, worn_place[i])
+            worn = placed([P, PICK], "worn%d" % i, WORN_OFFSET[i])
             nc.vector.tensor_tensor(out=worn[:], in0=looks[i][:], in1=wear_sb[:, i, :], op=ALU.subtract)
             nc.vector.tensor_tensor(
                 out=pages[i][:].indirect(pos2_sb[:]), in0=worn[:], in1=wgs_sb[:, i, :], op=ALU.mult
@@ -272,31 +289,31 @@ def tile_list_crease_bridge_features_kernel(
                     scale=row_values["gain"][:, i : i + 1],
                 )
 
-        by_w1 = [product(i, 2 * i, True) for i in range(3)]
-        by_w4 = [product(0, 6, False)]
-        times_depth(0, [acc[:] for acc in by_w1[0]], nc.vector)
+        w1_sums = [product(i, 2 * i, True) for i in range(PACK - 1)]
+        w4_sums = [product(0, 6, False)]
+        times_depth(0, [acc[:] for acc in w1_sums[0]], nc.vector)
         for i in (1, 2):
-            times_depth(i, bring_out(i, by_w1[i]), nc.gpsimd)
-        by_w4.append(product(1, 0, False))
-        features(0, by_w4[0])
-        last_by_w1 = bring_out(3, product(3, 4, True))
-        by_w4.append(product(2, 2, False))
-        by_w4.append(product(3, 6, False))
-        features(1, by_w4[1])
+            times_depth(i, bring_out(i, w1_sums[i]), nc.gpsimd)
+        w4_sums.append(product(1, 0, False))
+        features(0, w4_sums[0])
+        last_w1_sums = bring_out(3, product(3, 4, True))
+        w4_sums.append(product(2, 2, False))
+        w4_sums.append(product(3, 6, False))
+        features(1, w4_sums[1])
         rewrite(0)
-        times_depth(3, last_by_w1, nc.gpsimd)
-        features(2, by_w4[2])
+        times_depth(3, last_w1_sums, nc.gpsimd)
+        features(2, w4_sums[2])
         nc.scalar.copy(
             out=w3_codes[:].rearrange("p (i m) -> p i m", i=PACK),
             in_=w3_raw[:].rearrange("p (m i) -> p i m", i=PACK),
         )
         rewrite(1)
-        w3_scale = turns.tile([P, H], U8, name="w3_scale", offset=12 * KIB, align_bytes=64)
+        w3_scale = turns.tile([P, H], U8, name="w3_scale", offset=W3_SCALE_OFFSET, align_bytes=64)
         nc.gpsimd.tensor_copy(
             out=w3_scale[:].rearrange("p (i m) -> p i m", i=PACK),
             in_=w3_scale_raw[:].rearrange("p (m i) -> p i m", i=PACK),
         )
-        features(3, by_w4[3])
+        features(3, w4_sums[3])
         rewrite(2)
         rewrite(3)
 
@@ -313,13 +330,12 @@ def tile_list_crease_bridge_features_kernel(
             for i in range(PACK):
                 if i % per_bank == 0:
                     acc = bank(first_bank + i // per_bank, "read_out%d_%d" % (n, i))
-                place = acc[:, (i % per_bank) * width : (i % per_bank + 1) * width]
+                sums.append(acc[:, (i % per_bank) * width : (i % per_bank + 1) * width])
                 nc.tensor.matmul_mx(
-                    out=place, lhsT=w3_codes[:, i * P : (i + 1) * P].bitcast(FP8X4),
+                    out=sums[i], lhsT=w3_codes[:, i * P : (i + 1) * P].bitcast(FP8X4),
                     lhsT_scale=w3_scale[:, i * P : (i + 1) * P], rhs=codes[:].bitcast(FP8X4),
                     rhs_scale=scales[:], start=True, stop=True,
                 )
-                sums.append(place)
             return sums
 
         scaled = keep.tile([P, PACK, S], F32, name="scaled")
@@ -332,9 +348,29 @@ def tile_list_crease_bridge_features_kernel(
                     op=ALU.mult,
                 )
 
-        def plus_room(start, width, i, engine):
-            cols = slice(start, start + width)
+        def plus_room(c, i, engine):
+            cols = slice(c * BANK, (c + 1) * BANK)
             engine.tensor_tensor(out=room_sb[:, i, cols], in0=scaled[:, i, cols], in1=room_sb[:, i, cols], op=ALU.add)
+            nc.sync.dma_start(out=by_row(out)[:, i, cols], in_=room_sb[:, i, cols])
+
+        def plus_room_by_transposes(c, i, first_bank):
+            squares = range(BANK // P)
+            turned = bank(first_bank, "turned%d" % i)
+            for term, opens in ((room_sb, True), (scaled, False)):
+                for b in squares:
+                    nc.tensor.matmul(
+                        out=turned[:, b * P : (b + 1) * P],
+                        lhsT=term[:, i, c * BANK + b * P : c * BANK + (b + 1) * P],
+                        rhs=identity[:], is_transpose=True,
+                        start=(opens and b == 0), stop=(not opens and b == len(squares) - 1),
+                    )
+            turned_sb = keep.tile([P, BANK], F32, name="turned_sb%d" % i)
+            nc.scalar.copy(out=turned_sb[:], in_=turned[:])
+            back = bank(first_bank + 1, "back%d" % i)
+            for b in squares:
+                nc.tensor.transpose(back[:, b * P : (b + 1) * P], turned_sb[:, b * P : (b + 1) * P], identity[:])
+            cols = slice(c * BANK, (c + 1) * BANK)
+            nc.scalar.copy(out=room_sb[:, i, cols], in_=back[:])
             nc.sync.dma_start(out=by_row(out)[:, i, cols], in_=room_sb[:, i, cols])
 
         sums0 = read_out_products(0, 0, "codes0")
@@ -342,9 +378,10 @@ def tile_list_crease_bridge_features_kernel(
         times_h(0, sums0)
         sums2 = read_out_products(2, 4, "codes0")
         times_h(1, sums1)
-        for i in range(PACK - 1):
-            plus_room(0, BANK, i, nc.gpsimd)
+        plus_room(0, 0, nc.gpsimd)
+        plus_room_by_transposes(0, 1, 0)
+        plus_room(0, 2, nc.gpsimd)
+        plus_room_by_transposes(0, 3, 2)
         times_h(2, sums2)
-        plus_room(0, BANK, PACK - 1, nc.vector)
         for i in range(PACK):
-            plus_room(BANK, BANK, i, nc.vector)
+            plus_room(1, i, nc.vector)

from contextlib import ExitStack

import concourse.mybir as mybir
from concourse.masks import make_identity

K, T, S, PICK, H = 1536, 4096, 1024, 512, 512
FLOPS = 2 * 2 * K * H * S + 2 * H * H * S

F32 = mybir.dt.float32
BF16 = mybir.dt.bfloat16
I32 = mybir.dt.int32
U32 = mybir.dt.uint32
U16 = mybir.dt.uint16
U8 = mybir.dt.uint8
FP8X4 = mybir.dt.float8_e4m3fn_x4
FP4X4 = mybir.dt.float4_e2m1fn_x4
ACT = mybir.ActivationFunctionType
ALU = mybir.AluOpType
AXIS = mybir.AxisListType

P = 128
PACK = 4
PASSES = K // (P * PACK)
BLOCKS = 16
QUAD = 32
SCALE_ROWS = 4
QUAD_ORDER = (0, 2, 1, 3)
LIST_ROWS = 16
BANK = 512
KIB = 1024
TAB0_PIECES = 4
VECTOR_PITCH = 8
READ_OUT = ((0, 256), (256, 256), (512, 512))
H_OFFSET = (None, None, 0, 8 * KIB)
DEEP_OFFSET = (None, 2 * KIB, 10 * KIB, 4 * KIB)
WORN_OFFSET = (3 * KIB, 11 * KIB, 6 * KIB, None)
W3_SCALE_OFFSET = 12 * KIB


def tile_list_crease_bridge_features_kernel(
    tc, tab_words, tab_scales, offs, pos1, pos2, w1, w4_words, w4_scales, w3_words, w3_scales,
    depth, slope, share, wear, skip, wgs, gain, room, out,
):
    nc = tc.nc
    with ExitStack() as ctx:
        lists = ctx.enter_context(tc.tile_pool(name="lists", bufs=1))
        keep = ctx.enter_context(tc.tile_pool(name="keep", bufs=1))
        ring = ctx.enter_context(tc.tile_pool(name="ring", bufs=2))
        turns = ctx.enter_context(tc.tile_pool(name="turns", bufs=1))
        psum = ctx.enter_context(tc.psum_pool(name="psum", bufs=1))

        def bank(number, name):
            return psum.tile([P, BANK], F32, name=name, tag="bank%d" % number)

        def by_row(matrix):
            return matrix.rearrange("(p i) c -> p i c", i=PACK)

        tab_scale_rows = keep.tile([P, T], U8, name="tab_scale_rows", tag="chain_a", align_bytes=64)
        w4_scale_raw = keep.tile([P, PASSES, H], U8, name="w4_scale_raw", tag="chain_b", align_bytes=64)
        v_scales = keep.tile([P, PASSES, S], U8, name="v_scales", align_bytes=64)
        nc.vector.memset(tab_scale_rows[:].bitcast(I32), 0)
        nc.gpsimd.memset(w4_scale_raw[:].bitcast(I32), 0)
        nc.vector.memset(v_scales[:].bitcast(I32), 0)

        identity = keep.tile([P, P], F32, name="identity")
        make_identity(nc, identity[:])

        offs_sb = lists.tile([P, S // LIST_ROWS], U16, name="offs_sb")
        pos1_sb = lists.tile([P, PICK // LIST_ROWS], U16, name="pos1_sb")
        pos2_sb = lists.tile([P, PICK // LIST_ROWS], U16, name="pos2_sb")

        def load_tab(a, tag):
            words = keep.tile([P, T], U32, name="tab%d" % a, tag=tag, align_bytes=64)
            nc.sync.dma_start(out=words[:].bitcast(I32), in_=tab_words[a].rearrange("p t j -> p (t j)").bitcast(I32))
            return words

        def load_w1(a, tags):
            width = H // len(tags)
            parts = []
            for u, tag in enumerate(tags):
                part = keep.tile([P, PACK, width], F32, name="w1_raw%d_%d" % (a, u), tag=tag, align_bytes=64)
                rows = w1[P * PACK * a : P * PACK * (a + 1), u * width : (u + 1) * width]
                nc.sync.dma_start(out=part[:], in_=by_row(rows))
                parts.append(part)
            return parts

        tab = [keep.tile([P, T], U32, name="tab0", align_bytes=64)]
        tab0_words = tab_words[0].rearrange("p t j -> p (t j)").bitcast(I32)
        for u in range(TAB0_PIECES):
            cols = slice(u * T // TAB0_PIECES, (u + 1) * T // TAB0_PIECES)
            nc.sync.dma_start(out=tab[0][:, cols].bitcast(I32), in_=tab0_words[:, cols])
            if u == 0:
                nc.sync.dma_start(offs_sb[:], offs)
        w4_raw = keep.tile([P, PASSES, 2 * H], U8, name="w4_raw")
        nc.sync.dma_start(out=w4_raw[:].bitcast(I32), in_=w4_words.rearrange("a p c -> p a c").bitcast(I32))
        nc.sync.dma_start(pos1_sb[:], pos1)
        nc.sync.dma_start(pos2_sb[:], pos2)
        nc.sync.dma_start(
            out=tab_scale_rows[0 : 2 * PASSES * BLOCKS : 2, :].bitcast(I32),
            in_=tab_scales.rearrange("a q t -> q a t").bitcast(I32),
        )
        w1_raw = [load_w1(0, ["w1_raw0"])]
        for r in range(SCALE_ROWS):
            nc.sync.dma_start(
                out=w4_scale_raw[r:P:QUAD, :, :].bitcast(I32),
                in_=w4_scales[:, r:BLOCKS:SCALE_ROWS, :].rearrange("a q c -> q a c").bitcast(I32),
            )
        tab.append(load_tab(1, "chain_c"))

        picked_scale_rows = keep.tile([P, S], U8, name="picked_scale_rows")
        nc.vector.tensor_copy(out=picked_scale_rows[:], in_=tab_scale_rows[:].indirect(offs_sb[:]))
        w1_raw.append(load_w1(1, ["chain_a"]))
        span = 2 * SCALE_ROWS * PASSES
        for quad in QUAD_ORDER:
            nc.sync.dma_start(
                out=v_scales[QUAD * quad : QUAD * quad + SCALE_ROWS, :, :].bitcast(I32),
                in_=picked_scale_rows[span * quad : span * (quad + 1) : 2, :].bitcast(I32),
            )
        tab.append(load_tab(2, "chain_b"))
        w1_grouped = [
            keep.tile([P, PACK, P, PACK], BF16, name="w1_grouped%d" % a, tag="grouped%d" % a, align_bytes=64)
            for a in range(PASSES)
        ]

        w4_codes = keep.tile([P, PASSES, 2 * H], U8, name="w4_codes", align_bytes=64)
        w4_scale = keep.tile([P, PASSES, H], U8, name="w4_scale", align_bytes=64)
        w3_codes = keep.tile([P, H], U32, name="w3_codes", align_bytes=64)
        nc.vector.tensor_copy(
            out=w4_codes[:].bitcast(U16).rearrange("p a (i m) -> p a i m", i=PACK),
            in_=w4_raw[:].bitcast(U16).rearrange("p a (m i) -> p a i m", i=PACK),
        )
        nc.vector.tensor_copy(
            out=w4_scale[:].rearrange("p a (i m) -> p a i m", i=PACK),
            in_=w4_scale_raw[:].rearrange("p a (m i) -> p a i m", i=PACK),
        )

        v_codes, w1_codes, w1_scale = [], [], []

        def prepare_pass(a):
            picked = keep.tile([P, S], U32, name="v_codes%d" % a, align_bytes=64)
            nc.vector.tensor_copy(out=picked[:], in_=tab[a][:].indirect(offs_sb[:]))
            v_codes.append(picked)

            grouped = w1_grouped[a]
            n_parts = len(w1_raw[a])
            for u, part in enumerate(w1_raw[a]):
                m_cols = slice(u * P // n_parts, (u + 1) * P // n_parts)
                dealt = grouped[:, :, m_cols, :].rearrange("p i m j -> p m j i")
                source = part[:].rearrange("p j (m i) -> p m j i", i=PACK)
                if u == 0:
                    nc.scalar.copy(out=dealt, in_=source)
                else:
                    nc.vector.tensor_copy(out=dealt[:, :, :, 0], in_=source[:, :, :, 0])
                    nc.scalar.copy(out=dealt[:, :, :, 1:PACK], in_=source[:, :, :, 1:PACK])
            codes = keep.tile([P, H], U32, name="w1_codes%d" % a, align_bytes=64)
            scales = keep.tile([P, H], U8, name="w1_scale%d" % a, align_bytes=64)
            sets_at_once = PACK if a < PASSES - 1 else 1
            for i in range(0, PACK, sets_at_once):
                cols = slice(i * P, (i + sets_at_once) * P)
                nc.vector.quantize_mx(
                    out=codes[:, cols].bitcast(FP8X4), scales=scales[:, cols],
                    in_=grouped[:, i : i + sets_at_once, :, :].rearrange("p i m j -> p (i m j)"),
                )
            w1_codes.append(codes)
            w1_scale.append(scales)

        prepare_pass(0)
        w1_raw.append(load_w1(2, ["grouped0", "chain_c"]))

        vectors = (("slope", slope), ("share", share), ("skip", skip), ("gain", gain))
        depth_first = keep.tile(
            [P, 2 * S + len(vectors) * VECTOR_PITCH], F32, name="depth_first", tag="chain_a", align_bytes=64
        )
        depth_second = keep.tile([P, 2, S], F32, name="depth_second", tag="grouped0", align_bytes=64)
        depth_sb = [depth_first[:, 0:S], depth_first[:, S : 2 * S], depth_second[:, 0, :], depth_second[:, 1, :]]
        wear_wgs = keep.tile([P, 2, PACK, PICK], F32, name="wear_wgs", tag="chain_b", align_bytes=64)
        wear_sb = wear_wgs[:, 0, :, :]
        wgs_sb = wear_wgs[:, 1, :, :]
        nc.sync.dma_start(out=depth_sb[0], in_=by_row(depth)[:, 0, :])
        row_values = {}
        for number, (name, vector) in enumerate(vectors):
            first = 2 * S + VECTOR_PITCH * number
            row_values[name] = depth_first[:, first : first + PACK]
            nc.sync.dma_start(out=row_values[name], in_=vector.rearrange("(p i) -> p i", i=PACK))
        nc.sync.dma_start(out=depth_sb[1], in_=by_row(depth)[:, 1, :])
        nc.sync.dma_start(out=depth_sb[2], in_=by_row(depth)[:, 2, :])
        nc.sync.dma_start(out=wear_sb[:, 0, :], in_=by_row(wear)[:, 0, :])
        for quad in QUAD_ORDER:
            nc.sync.dma_start(out=wgs_sb[QUAD * quad : QUAD * (quad + 1), 0, :], in_=by_row(wgs)[:, 0, :])
        nc.sync.dma_start(out=depth_sb[3], in_=by_row(depth)[:, 3, :])
        for quad in QUAD_ORDER:
            nc.sync.dma_start(out=wgs_sb[QUAD * quad : QUAD * (quad + 1), 1:PACK, :], in_=by_row(wgs)[:, 1:PACK, :])
        nc.sync.dma_start(out=wear_sb[:, 1:PACK, :], in_=by_row(wear)[:, 1:PACK, :])

        prepare_pass(1)
        prepare_pass(2)
        top_factor = keep.tile([P, PACK], F32, name="top_factor")
        nc.vector.scalar_tensor_tensor(
            out=top_factor[:], in0=row_values["slope"], scalar=-1.0, in1=row_values["share"],
            op0=ALU.mult, op1=ALU.mult,
        )

        w3_scale_raw = keep.tile([P, H], U8, name="w3_scale_raw", tag="grouped1", align_bytes=64)
        nc.gpsimd.memset(w3_scale_raw[:].bitcast(I32), 0)
        for r in range(SCALE_ROWS):
            nc.sync.dma_start(
                out=w3_scale_raw[r:P:QUAD, :].bitcast(I32), in_=w3_scales[0, r:BLOCKS:SCALE_ROWS, :].bitcast(I32)
            )
        w3_raw = keep.tile([P, H], U32, name="w3_raw", tag="grouped2", align_bytes=64)
        nc.sync.dma_start(out=w3_raw[:].bitcast(I32), in_=w3_words[0].rearrange("p c j -> p (c j)").bitcast(I32))
        room_sb = keep.tile([P, PACK, S], F32, name="room_sb", tag="chain_c", align_bytes=64)
        nc.sync.dma_start(out=room_sb[:], in_=by_row(room))

        def placed(shape, name, offset):
            if offset is None:
                return keep.tile(shape, F32, name=name)
            return turns.tile(shape, F32, name=name, offset=offset)

        h = [placed([P, S], "h%d" % i, H_OFFSET[i]) for i in range(PACK)]
        deep = [placed([P, S], "deep%d" % i, DEEP_OFFSET[i]) for i in range(PACK)]
        top = keep.tile([P, PACK, S // BANK], F32, name="top")
        look_bias = keep.tile([P, PACK], F32, name="look_bias")
        page_grouped = [
            keep.tile([P, width, PACK], BF16, name="page_grouped%d" % n, align_bytes=64)
            for n, (start, width) in enumerate(READ_OUT)
        ]
        looks, pages = {}, {}

        halves = range(S // BANK)

        def product(i, first_bank, of_w1):
            cols = slice(i * P, (i + 1) * P)
            sums = [bank(first_bank + c, "sum%d_%d_%d" % (of_w1, i, c)) for c in halves]
            for a in range(PASSES):
                if of_w1:
                    codes, scales = w1_codes[a][:, cols].bitcast(FP8X4), w1_scale[a][:, cols]
                else:
                    codes, scales = w4_codes[:, a, 2 * i * P : 2 * (i + 1) * P].bitcast(FP4X4), w4_scale[:, a, cols]
                for c in halves:
                    j_cols = slice(c * BANK, (c + 1) * BANK)
                    nc.tensor.matmul_mx(
                        out=sums[c][:], lhsT=codes, lhsT_scale=scales, rhs=v_codes[a][:, j_cols].bitcast(FP8X4),
                        rhs_scale=v_scales[:, a, j_cols], start=(a == 0), stop=(a == PASSES - 1),
                    )
            return sums

        def bring_out(i, sums):
            copied = keep.tile([P, S], F32, name="w1_sums%d" % i)
            for c in halves:
                nc.scalar.copy(out=copied[:, c * BANK : (c + 1) * BANK], in_=sums[c][:])
            return [copied[:, c * BANK : (c + 1) * BANK] for c in halves]

        def times_depth(i, sums, engine):
            for c in halves:
                cols = slice(c * BANK, (c + 1) * BANK)
                engine.tensor_tensor(out=deep[i][:, cols], in0=sums[c], in1=depth_sb[i][:, cols], op=ALU.mult)

        def features(i, w4_sums):
            for c in halves:
                cols = slice(c * BANK, (c + 1) * BANK)
                nc.vector.tensor_tensor(out=h[i][:, cols], in0=w4_sums[c][:], in1=deep[i][:, cols], op=ALU.max)
            for c in halves:
                nc.vector.reduce_max(
                    out=top[:, i, c : c + 1], in_=h[i][:, c * BANK : (c + 1) * BANK], axis=AXIS.X
                )
            nc.vector.tensor_scalar(
                out=look_bias[:, i : i + 1], in0=top[:, i, 0:1], scalar1=top[:, i, 1:2],
                scalar2=top_factor[:, i : i + 1], op0=ALU.max, op1=ALU.mult,
            )
            looks[i] = ring.tile([P, PICK], F32, name="look%d" % i, tag="look")
            nc.scalar.activation(
                out=looks[i][:], in_=h[i][:].indirect(pos1_sb[:]), func=ACT.Sigmoid,
                bias=look_bias[:, i : i + 1], scale=row_values["slope"][:, i : i + 1],
            )
            pages[i] = ring.tile([P, S], F32, name="page%d" % i, tag="page", bufs=3)
            nc.scalar.activation(
                out=pages[i][:], in_=h[i][:], func=ACT.Copy, scale=row_values["skip"][:, i : i + 1]
            )

        def rewrite(i):
            worn = placed([P, PICK], "worn%d" % i, WORN_OFFSET[i])
            nc.vector.tensor_tensor(out=worn[:], in0=looks[i][:], in1=wear_sb[:, i, :], op=ALU.subtract)
            nc.vector.tensor_tensor(
                out=pages[i][:].indirect(pos2_sb[:]), in0=worn[:], in1=wgs_sb[:, i, :], op=ALU.mult
            )
            for n, (start, width) in enumerate(READ_OUT):
                nc.scalar.activation(
                    out=page_grouped[n][:, :, i], in_=pages[i][:, start : start + width], func=ACT.Copy,
                    scale=row_values["gain"][:, i : i + 1],
                )

        w1_sums = [product(i, 2 * i, True) for i in range(PACK - 1)]
        w4_sums = [product(0, 6, False)]
        times_depth(0, [acc[:] for acc in w1_sums[0]], nc.vector)
        for i in (1, 2):
            times_depth(i, bring_out(i, w1_sums[i]), nc.gpsimd)
        w4_sums.append(product(1, 0, False))
        features(0, w4_sums[0])
        last_w1_sums = bring_out(3, product(3, 4, True))
        w4_sums.append(product(2, 2, False))
        w4_sums.append(product(3, 6, False))
        features(1, w4_sums[1])
        rewrite(0)
        times_depth(3, last_w1_sums, nc.gpsimd)
        features(2, w4_sums[2])
        nc.scalar.copy(
            out=w3_codes[:].rearrange("p (i m) -> p i m", i=PACK),
            in_=w3_raw[:].rearrange("p (m i) -> p i m", i=PACK),
        )
        rewrite(1)
        w3_scale = turns.tile([P, H], U8, name="w3_scale", offset=W3_SCALE_OFFSET, align_bytes=64)
        nc.gpsimd.tensor_copy(
            out=w3_scale[:].rearrange("p (i m) -> p i m", i=PACK),
            in_=w3_scale_raw[:].rearrange("p (m i) -> p i m", i=PACK),
        )
        features(3, w4_sums[3])
        rewrite(2)
        rewrite(3)

        def read_out_products(n, first_bank, tag):
            start, width = READ_OUT[n]
            codes = keep.tile([P, width], U32, name="page_codes%d" % n, tag=tag, align_bytes=64)
            scales = keep.tile([P, width], U8, name="page_scale%d" % n, align_bytes=64)
            nc.vector.quantize_mx(
                out=codes[:].bitcast(FP8X4), scales=scales[:],
                in_=page_grouped[n][:].rearrange("p j i -> p (j i)"),
            )
            per_bank = BANK // width
            sums = []
            for i in range(PACK):
                if i % per_bank == 0:
                    acc = bank(first_bank + i // per_bank, "read_out%d_%d" % (n, i))
                sums.append(acc[:, (i % per_bank) * width : (i % per_bank + 1) * width])
                nc.tensor.matmul_mx(
                    out=sums[i], lhsT=w3_codes[:, i * P : (i + 1) * P].bitcast(FP8X4),
                    lhsT_scale=w3_scale[:, i * P : (i + 1) * P], rhs=codes[:].bitcast(FP8X4),
                    rhs_scale=scales[:], start=True, stop=True,
                )
            return sums

        scaled = keep.tile([P, PACK, S], F32, name="scaled")

        def times_h(n, sums):
            start, width = READ_OUT[n]
            for i in range(PACK):
                nc.vector.tensor_tensor(
                    out=scaled[:, i, start : start + width], in0=sums[i], in1=h[i][:, start : start + width],
                    op=ALU.mult,
                )

        def plus_room(c, i, engine):
            cols = slice(c * BANK, (c + 1) * BANK)
            engine.tensor_tensor(out=room_sb[:, i, cols], in0=scaled[:, i, cols], in1=room_sb[:, i, cols], op=ALU.add)
            nc.sync.dma_start(out=by_row(out)[:, i, cols], in_=room_sb[:, i, cols])

        def plus_room_by_transposes(c, i, first_bank):
            squares = range(BANK // P)
            turned = bank(first_bank, "turned%d" % i)
            for term, opens in ((room_sb, True), (scaled, False)):
                for b in squares:
                    nc.tensor.matmul(
                        out=turned[:, b * P : (b + 1) * P],
                        lhsT=term[:, i, c * BANK + b * P : c * BANK + (b + 1) * P],
                        rhs=identity[:], is_transpose=True,
                        start=(opens and b == 0), stop=(not opens and b == len(squares) - 1),
                    )
            turned_sb = keep.tile([P, BANK], F32, name="turned_sb%d" % i)
            nc.scalar.copy(out=turned_sb[:], in_=turned[:])
            back = bank(first_bank + 1, "back%d" % i)
            for b in squares:
                nc.tensor.transpose(back[:, b * P : (b + 1) * P], turned_sb[:, b * P : (b + 1) * P], identity[:])
            cols = slice(c * BANK, (c + 1) * BANK)
            nc.scalar.copy(out=room_sb[:, i, cols], in_=back[:])
            nc.sync.dma_start(out=by_row(out)[:, i, cols], in_=room_sb[:, i, cols])

        sums0 = read_out_products(0, 0, "codes0")
        sums1 = read_out_products(1, 2, "codes1")
        times_h(0, sums0)
        sums2 = read_out_products(2, 4, "codes0")
        times_h(1, sums1)
        plus_room(0, 0, nc.gpsimd)
        plus_room_by_transposes(0, 1, 0)
        plus_room(0, 2, nc.gpsimd)
        plus_room_by_transposes(0, 3, 2)
        times_h(2, sums2)
        for i in range(PACK):
            plus_room(1, i, nc.vector)
